import numpy as np
import ml_dtypes


def mxq(x, axis, fmt="e4m3"):
    dtype, down = {"e4m3": (ml_dtypes.float8_e4m3fn, 7), "e5m2": (ml_dtypes.float8_e5m2, 14)}[fmt]
    v = np.moveaxis(np.asarray(x, np.float32).astype(ml_dtypes.bfloat16).astype(np.float64), axis, -1)
    blocks = v.reshape(v.shape[:-1] + (-1, 32))
    amax = np.abs(blocks).max(-1, keepdims=True)
    byte = np.maximum(np.where(amax > 0, np.frexp(amax)[1] - 1 + 127, 0) - down, 1)
    scale = np.exp2(byte - 127.0)
    codes = (blocks / scale).astype(np.float32).astype(dtype).astype(np.float64)
    return np.moveaxis((codes * scale).reshape(v.shape), -1, axis)


WIDE = False


def mx_kscale(k):
    if not WIDE:
        return np.ones(k)
    levels = np.array([10, -10, 5, -5, 0])
    if k % 512:
        return np.exp2(np.random.permutation(np.resize(levels, k // 32))).repeat(32)
    a = np.empty((k // 512, 16))
    for p in range(k // 512):
        a[p, :8] = np.random.permutation(np.resize(levels, 8))
        for g in range(8):
            far = levels[np.abs(levels - a[p, g]) >= 10]
            a[p, g + 8] = far[np.random.randint(len(far))]
    return np.exp2(a.ravel()).repeat(32)


def f64(x):
    return np.asarray(x).astype(np.float64)


def striped8(idx):
    return np.asarray(idx).reshape(8, -1, 16).transpose(0, 2, 1).reshape(128, -1).astype(np.uint16)


def unstriped8(offs):
    return offs.reshape(8, 16, -1).transpose(0, 2, 1).reshape(8, -1).astype(np.int64)


def pick8(x, idx, run):
    r = np.arange(len(x))
    return x[r[:, None], idx[r % (8 * run) // run]]


E2M1 = np.array([0.0, 0.5, 1.0, 1.5, 2.0, 3.0, 4.0, 6.0, -0.0, -0.5, -1.0, -1.5, -2.0, -3.0, -4.0, -6.0])


def pack_weight(w, fmt):
    k, n = w.shape
    w = f64(np.asarray(w, np.float32).astype(ml_dtypes.bfloat16)).reshape(k // 32, 32, n)
    amax = np.abs(w).max(1)
    if fmt == "e4m3":
        byte = np.frexp(amax)[1] - 1 + 127 - 7
    else:
        mant, ex = np.frexp(amax / 6.0)
        byte = np.where(mant > 0.5, ex, ex - 1) + 127
    byte = np.clip(np.where(amax > 0, byte, 1), 1, 254)
    scaled = (w * np.exp2(127.0 - byte)[:, None, :]).reshape(k, n).astype(np.float32)
    by_word = np.ascontiguousarray(scaled.reshape(k // 512, 128, 4, n).transpose(0, 1, 3, 2))
    if fmt == "e4m3":
        words = by_word.astype(ml_dtypes.float8_e4m3fn).view(np.uint8)
    else:
        c = by_word.astype(ml_dtypes.float4_e2m1fn).view(np.uint8) & 0xF
        words = (c[..., 0::2] | (c[..., 1::2] << 4)).reshape(k // 512, 128, 2 * n)
    return np.ascontiguousarray(words), np.ascontiguousarray(byte.astype(np.uint8).reshape(k // 512, 16, n))


def unpack_weight(words, scales, fmt):
    g, _, n = scales.shape
    words = np.ascontiguousarray(words).reshape(g, 128, n, -1)
    if fmt == "e4m3":
        vals = words.view(ml_dtypes.float8_e4m3fn).astype(np.float64)
    else:
        nib = np.empty((g, 128, n, 4), np.uint8)
        nib[..., 0::2] = words & 0xF
        nib[..., 1::2] = words >> 4
        vals = E2M1[nib]
    vals = vals * np.repeat(np.exp2(scales.astype(np.float64) - 127.0), 8, axis=1)[..., None]
    return vals.transpose(0, 1, 3, 2).reshape(g * 512, n)


D, T, I, Q = 512, 1024, 512, 128


def setup_inputs():
    n = np.random.standard_normal
    idx = np.stack([np.random.permutation(T)[:I] for _ in range(8)])
    idx2 = np.stack([np.random.permutation(T)[:I] for _ in range(8)])
    idx3 = np.stack([np.random.permutation(T)[:I] for _ in range(8)])
    fd = mx_kscale(D)
    keysp = pack_weight(n((D, T)) / fd[:, None], "e2m1")
    return {
        "query": (n((D, Q)) * 1.0 / np.sqrt(D) * fd[:, None]).astype(np.float32),
        "keys_words": keysp[0],
        "keys_scales": keysp[1],
        "old": (1.0 * n((Q, T))).astype(np.float32),
        "share2": (np.random.uniform(0.4, 1.2, (Q, 1))).astype(np.float32),
        "offs": striped8(idx),
        "offs2": striped8(idx2),
        "offs3": striped8(idx3),
    }


def reference(query, keys_words, keys_scales, old, share2, offs, offs2, offs3):
    idx = unstriped8(offs)
    idx2 = unstriped8(offs2)
    idx3 = unstriped8(offs3)
    keysu = unpack_weight(keys_words, keys_scales, "e2m1")
    queryq = mxq(f64(query), 0, "e4m3")
    a = queryq.T @ keysu
    w = pick8(a, idx, 16) * pick8(a, idx2, 16)
    f1 = np.zeros((Q, T))
    f1[np.arange(Q)[:, None], idx[np.arange(Q) % 128 // 16]] = w
    f2 = np.zeros((Q, T))
    f2[np.arange(Q)[:, None], idx3[np.arange(Q) % 128 // 16]] = w
    y = f64(old) + f1 + f2 * f64(share2)
    return y

@@ -1,0 +1,136 @@
+from contextlib import ExitStack
+
+import concourse.mybir as mybir
+from concourse.masks import make_identity
+
+D, T, SLOTS, Q = 512, 1024, 512, 128
+FLOPS = 2 * D * T * Q
+
+F32 = mybir.dt.float32
+BF16 = mybir.dt.bfloat16
+I32 = mybir.dt.int32
+U32 = mybir.dt.uint32
+U16 = mybir.dt.uint16
+U8 = mybir.dt.uint8
+FP8X4 = mybir.dt.float8_e4m3fn_x4
+FP4X4 = mybir.dt.float4_e2m1fn_x4
+MULT = mybir.AluOpType.mult
+ADD = mybir.AluOpType.add
+COPY = mybir.ActivationFunctionType.Copy
+
+P = 128
+PACK = 4
+PIECES = 4
+PIECE = T // PIECES
+BLOCKS = PIECE // P
+HALF = SLOTS // 2
+LIST_COLS = SLOTS // 16
+
+
+def tile_attend_pairproduct_lean_twiceput_heads_kernel(
+    tc, query, keys_words, keys_scales, old, share2, offs, offs2, offs3, out
+):
+    nc = tc.nc
+    with ExitStack() as ctx:
+        sb = ctx.enter_context(tc.tile_pool(name="sb", bufs=1))
+        ps = ctx.enter_context(tc.psum_pool(name="ps", bufs=1))
+
+        k_scales = sb.tile([P, T], U8, align_bytes=64)
+
+        q_raw = sb.tile([P, PACK, Q], F32)
+        nc.sync.dma_start(out=q_raw[:], in_=query.rearrange("(p j) q -> p j q", j=PACK))
+        k_words = sb.tile([P, 2 * T], U8, align_bytes=64)
+        nc.sync.dma_start(out=k_words[:].bitcast(I32), in_=keys_words[0].bitcast(I32))
+        for quad in range(4):
+            nc.scalar.dma_start(
+                out=k_scales[32 * quad : 32 * quad + 4, :].bitcast(I32),
+                in_=keys_scales[0, 4 * quad : 4 * quad + 4, :].bitcast(I32),
+            )
+        list1 = sb.tile([P, LIST_COLS], U16)
+        nc.sync.dma_start(list1[:], offs)
+        list2 = sb.tile([P, LIST_COLS], U16)
+        nc.sync.dma_start(list2[:], offs2)
+        old_sb = sb.tile([P, T], F32)
+        nc.sync.dma_start(out=old_sb[:], in_=old)
+        list3 = sb.tile([P, LIST_COLS], U16)
+        nc.sync.dma_start(list3[:], offs3)
+        share = sb.tile([P, 1], F32)
+        nc.sync.dma_start(out=share[:], in_=share2)
+
+        first_puts = [sb.tile([P, T], F32, name=f"first_put{h}") for h in range(2)]
+        second_put = sb.tile([P, T], F32)
+        for window in first_puts:
+            nc.vector.memset(window[:], 0.0)
+        nc.vector.memset(second_put[:], 0.0)
+        ident = sb.tile([P, P], F32)
+        make_identity(nc, ident[:])
+
+        q_bf = sb.tile([P, Q, PACK], BF16, align_bytes=64)
+        nc.vector.tensor_copy(out=q_bf[:], in_=q_raw[:].rearrange("p j q -> p q j"))
+        q_codes = sb.tile([P, Q], U32, align_bytes=64)
+        q_scales = sb.tile([P, Q], U8, align_bytes=64)
+        nc.vector.quantize_mx(
+            out=q_codes[:].bitcast(FP8X4),
+            scales=q_scales[:],
+            in_=q_bf[:].rearrange("p q j -> p (q j)"),
+        )
+
+        scores = sb.tile([P, T], F32)
+        for b in range(PIECES):
+            cols = slice(b * PIECE, (b + 1) * PIECE)
+            acc = ps.tile([P, PIECE], F32, name=f"acc{b}", tag=f"left{b}")
+            nc.tensor.matmul_mx(
+                out=acc[:],
+                lhsT=q_codes[:].bitcast(FP8X4),
+                lhsT_scale=q_scales[:],
+                rhs=k_words[:, 2 * b * PIECE : 2 * (b + 1) * PIECE].bitcast(FP4X4),
+                rhs_scale=k_scales[:, cols],
+                start=True,
+                stop=True,
+            )
+            if b % 2 == 0:
+                nc.scalar.copy(out=scores[:, cols], in_=acc[:])
+            else:
+                nc.vector.tensor_copy(out=scores[:, cols], in_=acc[:])
+
+        slots = [slice(0, HALF), slice(HALF, SLOTS)]
+        entries = [slice(0, LIST_COLS // 2), slice(LIST_COLS // 2, LIST_COLS)]
+        left = sb.tile([P, SLOTS], F32)
+        right = sb.tile([P, SLOTS], F32)
+        nc.scalar.activation(left[:, slots[0]], scores[:].indirect(list1[:, entries[0]]), COPY)
+        nc.vector.tensor_copy(right[:, slots[0]], scores[:].indirect(list2[:, entries[0]]))
+        nc.scalar.activation(left[:, slots[1]], scores[:].indirect(list1[:, entries[1]]), COPY)
+        nc.scalar.activation(right[:, slots[1]], scores[:].indirect(list2[:, entries[1]]), COPY)
+
+        for h in range(2):
+            nc.vector.tensor_tensor(
+                first_puts[h][:].indirect(list1[:, entries[h]]), left[:, slots[h]], right[:, slots[h]], MULT
+            )
+        nc.vector.tensor_tensor(second_put[:].indirect(list3[:]), left[:], right[:], MULT)
+
+        addends = [old_sb] + first_puts
+        turned = [ps.tile([P, BLOCKS, P], F32, name=f"turned{b}", tag=f"left{b}") for b in range(PIECES)]
+        for n, addend in enumerate(addends):
+            for b in range(PIECES):
+                for j in range(BLOCKS):
+                    c0 = b * PIECE + j * P
+                    nc.tensor.matmul(
+                        turned[b][:, j, :],
+                        addend[:, c0 : c0 + P],
+                        ident[:],
+                        start=(n == 0 and j == 0),
+                        stop=(n == len(addends) - 1 and j == BLOCKS - 1),
+                        is_transpose=True,
+                    )
+        result = sb.tile([P, T], F32)
+        for b in range(PIECES):
+            cols = slice(b * PIECE, (b + 1) * PIECE)
+            turned_sb = sb.tile([P, BLOCKS, P], F32, name=f"turned_sb{b}")
+            nc.scalar.copy(out=turned_sb[:], in_=turned[b][:])
+            partial = ps.tile([P, PIECE], F32, name=f"partial{b}", tag=f"right{b}")
+            for j in range(BLOCKS):
+                nc.tensor.transpose(partial[:, j * P : (j + 1) * P], turned_sb[:, j, :], ident[:])
+            nc.vector.scalar_tensor_tensor(
+                result[:, cols], second_put[:, cols], share[:], partial[:], MULT, ADD
+            )
+            nc.sync.dma_start(out=out[:, cols], in_=result[:, cols])

@@ -23,7 +23,7 @@ PACK = 4
 PIECES = 4
 PIECE = T // PIECES
 BLOCKS = PIECE // P
-HALF = SLOTS // 2
+HEAD = 128
 LIST_COLS = SLOTS // 16
 
 
@@ -57,33 +57,41 @@ def tile_attend_pairproduct_lean_twiceput_heads_kernel(
         share = sb.tile([P, 1], F32)
         nc.sync.dma_start(out=share[:], in_=share2)
 
-        first_puts = [sb.tile([P, T], F32, name=f"first_put{h}") for h in range(2)]
+        first_puts = [sb.tile([P, T], F32, name=f"first_put{h}") for h in range(1)]
         second_put = sb.tile([P, T], F32)
         for window in first_puts:
             nc.vector.memset(window[:], 0.0)
         nc.vector.memset(second_put[:], 0.0)
+        ones = sb.tile([P, HEAD], F32)
+        nc.gpsimd.memset(ones[:], 1.0)
         ident = sb.tile([P, P], F32)
         make_identity(nc, ident[:])
 
         q_bf = sb.tile([P, Q, PACK], BF16, align_bytes=64)
-        nc.vector.tensor_copy(out=q_bf[:], in_=q_raw[:].rearrange("p j q -> p q j"))
+        for h in range(2):
+            rows = slice(h * Q // 2, (h + 1) * Q // 2)
+            nc.vector.tensor_copy(out=q_bf[:, rows, :], in_=q_raw[:, :, rows].rearrange("p j q -> p q j"))
         q_codes = sb.tile([P, Q], U32, align_bytes=64)
         q_scales = sb.tile([P, Q], U8, align_bytes=64)
-        nc.vector.quantize_mx(
-            out=q_codes[:].bitcast(FP8X4),
-            scales=q_scales[:],
-            in_=q_bf[:].rearrange("p q j -> p (q j)"),
-        )
+        for h in range(2):
+            rows = slice(h * Q // 2, (h + 1) * Q // 2)
+            nc.vector.quantize_mx(
+                out=q_codes[:, rows].bitcast(FP8X4),
+                scales=q_scales[:, rows],
+                in_=q_bf[:, rows, :].rearrange("p q j -> p (q j)"),
+            )
 
         scores = sb.tile([P, T], F32)
-        for b in range(PIECES):
-            cols = slice(b * PIECE, (b + 1) * PIECE)
-            acc = ps.tile([P, PIECE], F32, name=f"acc{b}", tag=f"left{b}")
+        widths = [256,256,256,128,128]
+        for b, width in enumerate(widths):
+            c0 = sum(widths[:b])
+            cols = slice(c0, c0 + width)
+            acc = ps.tile([P, width], F32, name=f"acc{b}", tag=f"bank{b}")
             nc.tensor.matmul_mx(
                 out=acc[:],
                 lhsT=q_codes[:].bitcast(FP8X4),
                 lhsT_scale=q_scales[:],
-                rhs=k_words[:, 2 * b * PIECE : 2 * (b + 1) * PIECE].bitcast(FP4X4),
+                rhs=k_words[:, 2 * c0 : 2 * (c0 + width)].bitcast(FP4X4),
                 rhs_scale=k_scales[:, cols],
                 start=True,
                 stop=True,
@@ -93,23 +101,24 @@ def tile_attend_pairproduct_lean_twiceput_heads_kernel(
             else:
                 nc.vector.tensor_copy(out=scores[:, cols], in_=acc[:])
 
-        slots = [slice(0, HALF), slice(HALF, SLOTS)]
-        entries = [slice(0, LIST_COLS // 2), slice(LIST_COLS // 2, LIST_COLS)]
+        slots = [slice(0, HEAD), slice(HEAD, SLOTS)]
+        entries = [slice(0, HEAD // 16), slice(HEAD // 16, LIST_COLS)]
         left = sb.tile([P, SLOTS], F32)
         right = sb.tile([P, SLOTS], F32)
-        nc.scalar.activation(left[:, slots[0]], scores[:].indirect(list1[:, entries[0]]), COPY)
-        nc.vector.tensor_copy(right[:, slots[0]], scores[:].indirect(list2[:, entries[0]]))
+        nc.vector.tensor_tensor(left[:, slots[0]], scores[:].indirect(list1[:, entries[0]]), ones[:], MULT)
+        nc.vector.tensor_tensor(right[:, slots[0]], scores[:].indirect(list2[:, entries[0]]), ones[:], MULT)
         nc.scalar.activation(left[:, slots[1]], scores[:].indirect(list1[:, entries[1]]), COPY)
         nc.scalar.activation(right[:, slots[1]], scores[:].indirect(list2[:, entries[1]]), COPY)
-
         for h in range(2):
             nc.vector.tensor_tensor(
-                first_puts[h][:].indirect(list1[:, entries[h]]), left[:, slots[h]], right[:, slots[h]], MULT
+                first_puts[0][:].indirect(list1[:, entries[h]]), left[:, slots[h]], right[:, slots[h]], MULT
             )
-        nc.vector.tensor_tensor(second_put[:].indirect(list3[:]), left[:], right[:], MULT)
+            nc.vector.tensor_tensor(
+                second_put[:].indirect(list3[:, entries[h]]), left[:, slots[h]], right[:, slots[h]], MULT
+            )
 
         addends = [old_sb] + first_puts
-        turned = [ps.tile([P, BLOCKS, P], F32, name=f"turned{b}", tag=f"left{b}") for b in range(PIECES)]
+        turned = [ps.tile([P, BLOCKS, P], F32, name=f"turned{b}", tag=f"bank{b}") for b in range(PIECES)]
         for n, addend in enumerate(addends):
             for b in range(PIECES):
                 for j in range(BLOCKS):
@@ -127,7 +136,7 @@ def tile_attend_pairproduct_lean_twiceput_heads_kernel(
             cols = slice(b * PIECE, (b + 1) * PIECE)
             turned_sb = sb.tile([P, BLOCKS, P], F32, name=f"turned_sb{b}")
             nc.scalar.copy(out=turned_sb[:], in_=turned[b][:])
-            partial = ps.tile([P, PIECE], F32, name=f"partial{b}", tag=f"right{b}")
+            partial = ps.tile([P, PIECE], F32, name=f"partial{b}", tag=f"bank{PIECES + b}")
             for j in range(BLOCKS):
                 nc.tensor.transpose(partial[:, j * P : (j + 1) * P], turned_sb[:, j, :], ident[:])
             nc.vector.scalar_tensor_tensor(

@@ -39,13 +39,13 @@ def tile_attend_pairproduct_lean_twiceput_heads_kernel(
 
         q_raw = sb.tile([P, PACK, Q], F32)
         nc.sync.dma_start(out=q_raw[:], in_=query.rearrange("(p j) q -> p j q", j=PACK))
-        k_words = sb.tile([P, 2 * T], U8, align_bytes=64)
-        nc.sync.dma_start(out=k_words[:].bitcast(I32), in_=keys_words[0].bitcast(I32))
         for quad in range(4):
-            nc.scalar.dma_start(
+            nc.sync.dma_start(
                 out=k_scales[32 * quad : 32 * quad + 4, :].bitcast(I32),
                 in_=keys_scales[0, 4 * quad : 4 * quad + 4, :].bitcast(I32),
             )
+        k_words = sb.tile([P, 2 * T], U8, align_bytes=64)
+        nc.sync.dma_start(out=k_words[:].bitcast(I32), in_=keys_words[0].bitcast(I32))
         list1 = sb.tile([P, LIST_COLS], U16)
         nc.sync.dma_start(list1[:], offs)
         list2 = sb.tile([P, LIST_COLS], U16)
@@ -96,7 +96,7 @@ def tile_attend_pairproduct_lean_twiceput_heads_kernel(
                 start=True,
                 stop=True,
             )
-            if b % 2 == 0:
+            if b % 2 == 1:
                 nc.scalar.copy(out=scores[:, cols], in_=acc[:])
             else:
                 nc.vector.tensor_copy(out=scores[:, cols], in_=acc[:])
@@ -139,7 +139,10 @@ def tile_attend_pairproduct_lean_twiceput_heads_kernel(
             partial = ps.tile([P, PIECE], F32, name=f"partial{b}", tag=f"bank{PIECES + b}")
             for j in range(BLOCKS):
                 nc.tensor.transpose(partial[:, j * P : (j + 1) * P], turned_sb[:, j, :], ident[:])
-            nc.vector.scalar_tensor_tensor(
-                result[:, cols], second_put[:, cols], share[:], partial[:], MULT, ADD
-            )
-            nc.sync.dma_start(out=out[:, cols], in_=result[:, cols])
+            step = P if b == PIECES - 1 else PIECE
+            for s0 in range(0, PIECE, step):
+                part = slice(b * PIECE + s0, b * PIECE + s0 + step)
+                nc.vector.scalar_tensor_tensor(
+                    result[:, part], second_put[:, part], share[:], partial[:, s0 : s0 + step], MULT, ADD
+                )
+                nc.sync.dma_start(out=out[:, part], in_=result[:, part])

from contextlib import ExitStack

import concourse.mybir as mybir
from concourse.masks import make_identity

D, T, SLOTS, Q = 512, 1024, 512, 128
FLOPS = 2 * D * T * Q

F32 = mybir.dt.float32
BF16 = mybir.dt.bfloat16
I32 = mybir.dt.int32
U32 = mybir.dt.uint32
U16 = mybir.dt.uint16
U8 = mybir.dt.uint8
FP8X4 = mybir.dt.float8_e4m3fn_x4
FP4X4 = mybir.dt.float4_e2m1fn_x4
MULT = mybir.AluOpType.mult
ADD = mybir.AluOpType.add
COPY = mybir.ActivationFunctionType.Copy

P = 128
PACK = 4
PIECES = 4
PIECE = T // PIECES
BLOCKS = PIECE // P
HEAD = 128
LIST_COLS = SLOTS // 16


def tile_attend_pairproduct_lean_twiceput_heads_kernel(
    tc, query, keys_words, keys_scales, old, share2, offs, offs2, offs3, out
):
    nc = tc.nc
    with ExitStack() as ctx:
        sb = ctx.enter_context(tc.tile_pool(name="sb", bufs=1))
        ps = ctx.enter_context(tc.psum_pool(name="ps", bufs=1))

        k_scales = sb.tile([P, T], U8, align_bytes=64)

        q_raw = sb.tile([P, PACK, Q], F32)
        nc.sync.dma_start(out=q_raw[:], in_=query.rearrange("(p j) q -> p j q", j=PACK))
        for quad in range(4):
            nc.sync.dma_start(
                out=k_scales[32 * quad : 32 * quad + 4, :].bitcast(I32),
                in_=keys_scales[0, 4 * quad : 4 * quad + 4, :].bitcast(I32),
            )
        k_words = sb.tile([P, 2 * T], U8, align_bytes=64)
        nc.sync.dma_start(out=k_words[:].bitcast(I32), in_=keys_words[0].bitcast(I32))
        list1 = sb.tile([P, LIST_COLS], U16)
        nc.sync.dma_start(list1[:], offs)
        list2 = sb.tile([P, LIST_COLS], U16)
        nc.sync.dma_start(list2[:], offs2)
        old_sb = sb.tile([P, T], F32)
        nc.sync.dma_start(out=old_sb[:], in_=old)
        list3 = sb.tile([P, LIST_COLS], U16)
        nc.sync.dma_start(list3[:], offs3)
        share = sb.tile([P, 1], F32)
        nc.sync.dma_start(out=share[:], in_=share2)

        first_puts = [sb.tile([P, T], F32, name=f"first_put{h}") for h in range(1)]
        second_put = sb.tile([P, T], F32)
        for window in first_puts:
            nc.vector.memset(window[:], 0.0)
        nc.vector.memset(second_put[:], 0.0)
        ones = sb.tile([P, HEAD], F32)
        nc.gpsimd.memset(ones[:], 1.0)
        ident = sb.tile([P, P], F32)
        make_identity(nc, ident[:])

        q_bf = sb.tile([P, Q, PACK], BF16, align_bytes=64)
        for h in range(2):
            rows = slice(h * Q // 2, (h + 1) * Q // 2)
            nc.vector.tensor_copy(out=q_bf[:, rows, :], in_=q_raw[:, :, rows].rearrange("p j q -> p q j"))
        q_codes = sb.tile([P, Q], U32, align_bytes=64)
        q_scales = sb.tile([P, Q], U8, align_bytes=64)
        for h in range(2):
            rows = slice(h * Q // 2, (h + 1) * Q // 2)
            nc.vector.quantize_mx(
                out=q_codes[:, rows].bitcast(FP8X4),
                scales=q_scales[:, rows],
                in_=q_bf[:, rows, :].rearrange("p q j -> p (q j)"),
            )

        scores = sb.tile([P, T], F32)
        widths = [256,256,256,128,128]
        for b, width in enumerate(widths):
            c0 = sum(widths[:b])
            cols = slice(c0, c0 + width)
            acc = ps.tile([P, width], F32, name=f"acc{b}", tag=f"bank{b}")
            nc.tensor.matmul_mx(
                out=acc[:],
                lhsT=q_codes[:].bitcast(FP8X4),
                lhsT_scale=q_scales[:],
                rhs=k_words[:, 2 * c0 : 2 * (c0 + width)].bitcast(FP4X4),
                rhs_scale=k_scales[:, cols],
                start=True,
                stop=True,
            )
            if b % 2 == 1:
                nc.scalar.copy(out=scores[:, cols], in_=acc[:])
            else:
                nc.vector.tensor_copy(out=scores[:, cols], in_=acc[:])

        slots = [slice(0, HEAD), slice(HEAD, SLOTS)]
        entries = [slice(0, HEAD // 16), slice(HEAD // 16, LIST_COLS)]
        left = sb.tile([P, SLOTS], F32)
        right = sb.tile([P, SLOTS], F32)
        nc.vector.tensor_tensor(left[:, slots[0]], scores[:].indirect(list1[:, entries[0]]), ones[:], MULT)
        nc.vector.tensor_tensor(right[:, slots[0]], scores[:].indirect(list2[:, entries[0]]), ones[:], MULT)
        nc.scalar.activation(left[:, slots[1]], scores[:].indirect(list1[:, entries[1]]), COPY)
        nc.scalar.activation(right[:, slots[1]], scores[:].indirect(list2[:, entries[1]]), COPY)
        for h in range(2):
            nc.vector.tensor_tensor(
                first_puts[0][:].indirect(list1[:, entries[h]]), left[:, slots[h]], right[:, slots[h]], MULT
            )
            nc.vector.tensor_tensor(
                second_put[:].indirect(list3[:, entries[h]]), left[:, slots[h]], right[:, slots[h]], MULT
            )

        addends = [old_sb] + first_puts
        turned = [ps.tile([P, BLOCKS, P], F32, name=f"turned{b}", tag=f"bank{b}") for b in range(PIECES)]
        for n, addend in enumerate(addends):
            for b in range(PIECES):
                for j in range(BLOCKS):
                    c0 = b * PIECE + j * P
                    nc.tensor.matmul(
                        turned[b][:, j, :],
                        addend[:, c0 : c0 + P],
                        ident[:],
                        start=(n == 0 and j == 0),
                        stop=(n == len(addends) - 1 and j == BLOCKS - 1),
                        is_transpose=True,
                    )
        result = sb.tile([P, T], F32)
        for b in range(PIECES):
            cols = slice(b * PIECE, (b + 1) * PIECE)
            turned_sb = sb.tile([P, BLOCKS, P], F32, name=f"turned_sb{b}")
            nc.scalar.copy(out=turned_sb[:], in_=turned[b][:])
            partial = ps.tile([P, PIECE], F32, name=f"partial{b}", tag=f"bank{PIECES + b}")
            for j in range(BLOCKS):
                nc.tensor.transpose(partial[:, j * P : (j + 1) * P], turned_sb[:, j, :], ident[:])
            step = P if b == PIECES - 1 else PIECE
            for s0 in range(0, PIECE, step):
                part = slice(b * PIECE + s0, b * PIECE + s0 + step)
                nc.vector.scalar_tensor_tensor(
                    result[:, part], second_put[:, part], share[:], partial[:, s0 : s0 + step], MULT, ADD
                )
                nc.sync.dma_start(out=out[:, part], in_=result[:, part])
